import numpy as np
import ml_dtypes

BF16 = ml_dtypes.bfloat16


def bf(x):
    return np.asarray(x, np.float32).astype(BF16)


def f32(x):
    return np.asarray(x, np.float32)


def f64(x):
    return np.asarray(x).astype(np.float64)


def striped(idx):
    return np.concatenate([l.reshape(-1, 16).T for l in idx])


def rows(idx, k):
    return np.tile(np.repeat(idx, 16, axis=0), (k // (16 * 8), 1))


def look(tab, idx):
    return np.take_along_axis(f64(tab), rows(idx, len(tab)), axis=1)


K, S, V, N, M = 128, 2048, 2048, 2048, 128


def setup_inputs():
    return {"tab": f32(np.random.standard_normal((K, S))), "qry": f32(np.random.standard_normal((K, V))), "w": bf(np.random.uniform(0.0, 1.0, (K, M)) / K), "offs": striped(np.random.randint(0, S, (8, N)))}


def reference(tab, qry, w, offs):
    idx = np.stack([g.T.reshape(-1) for g in np.split(offs, 8)])
    x = np.abs(look(tab, idx) - f64(qry))
    y = f64(w).T @ x
    return np.exp(-y)

@@ -1,0 +1,42 @@
+import concourse.mybir as mybir
+
+P = 128
+N = 2048
+PIECE = 512
+GROUP = 16
+F32, BF16, U16 = mybir.dt.float32, mybir.dt.bfloat16, mybir.dt.uint16
+ACT = mybir.ActivationFunctionType
+FLOPS = 2 * P * P * N
+
+
+def tile_lookup_manh_sub_rbf_kernel(tc, tab, qry, w, offs, out):
+    nc = tc.nc
+    pieces = N // PIECE
+    with (
+        tc.tile_pool(name="held", bufs=1) as held,
+        tc.tile_pool(name="work", bufs=pieces) as work,
+        tc.psum_pool(name="psum", bufs=pieces) as psum,
+    ):
+        offsets = held.tile([P, N // GROUP], U16, name="offsets")
+        table = held.tile([P, tab.shape[1]], F32, name="table")
+        weights = held.tile([P, P], BF16, name="weights")
+        nc.sync.dma_start(offsets[:], offs)
+        nc.sync.dma_start(table[:], tab)
+        queries = []
+        for i in range(pieces):
+            query = work.tile([P, PIECE], F32, name="query")
+            nc.sync.dma_start(query[:], qry[:, i * PIECE:(i + 1) * PIECE])
+            queries.append(query)
+        nc.scalar.dma_start(weights[:], w)
+
+        for i in range(pieces):
+            entries = offsets[:, i * PIECE // GROUP:(i + 1) * PIECE // GROUP]
+            diff = work.tile([P, PIECE], F32, name="diff")
+            nc.vector.tensor_tensor(diff[:], table[:].indirect(entries), queries[i][:], mybir.AluOpType.subtract)
+            x = work.tile([P, PIECE], BF16, name="x")
+            nc.scalar.activation(x[:], diff[:], ACT.Abs)
+            dist = psum.tile([P, PIECE], F32, name="dist")
+            nc.tensor.matmul(dist[:], weights[:], x[:], start=True, stop=True)
+            result = work.tile([P, PIECE], F32, name="result")
+            nc.scalar.activation(result[:], dist[:], ACT.Exp, scale=-1.0)
+            nc.sync.dma_start(out[:, i * PIECE:(i + 1) * PIECE], result[:])

@@ -3,40 +3,63 @@ import concourse.mybir as mybir
 P = 128
 N = 2048
 PIECE = 512
+HALF = PIECE // 2
 GROUP = 16
 F32, BF16, U16 = mybir.dt.float32, mybir.dt.bfloat16, mybir.dt.uint16
 ACT = mybir.ActivationFunctionType
+ALU = mybir.AluOpType
 FLOPS = 2 * P * P * N
 
 
 def tile_lookup_manh_sub_rbf_kernel(tc, tab, qry, w, offs, out):
     nc = tc.nc
     pieces = N // PIECE
+    last = pieces - 1
     with (
         tc.tile_pool(name="held", bufs=1) as held,
-        tc.tile_pool(name="work", bufs=pieces) as work,
-        tc.psum_pool(name="psum", bufs=pieces) as psum,
+        tc.tile_pool(name="work", bufs=pieces + 1) as work,
+        tc.psum_pool(name="psum", bufs=pieces + 1) as psum,
     ):
         offsets = held.tile([P, N // GROUP], U16, name="offsets")
         table = held.tile([P, tab.shape[1]], F32, name="table")
         weights = held.tile([P, P], BF16, name="weights")
-        nc.sync.dma_start(offsets[:], offs)
+        queries = [work.tile([P, PIECE], F32, name="query") for i in range(pieces)]
         nc.sync.dma_start(table[:], tab)
-        queries = []
-        for i in range(pieces):
-            query = work.tile([P, PIECE], F32, name="query")
-            nc.sync.dma_start(query[:], qry[:, i * PIECE:(i + 1) * PIECE])
-            queries.append(query)
-        nc.scalar.dma_start(weights[:], w)
+        nc.sync.dma_start(offsets[:], offs)
+        nc.sync.dma_start(queries[0][:], qry[:, 0:PIECE])
+        nc.sync.dma_start(weights[:], w)
+        for i in range(1, pieces):
+            nc.sync.dma_start(queries[i][:], qry[:, i * PIECE:(i + 1) * PIECE])
 
-        for i in range(pieces):
+        def difference(i):
             entries = offsets[:, i * PIECE // GROUP:(i + 1) * PIECE // GROUP]
             diff = work.tile([P, PIECE], F32, name="diff")
-            nc.vector.tensor_tensor(diff[:], table[:].indirect(entries), queries[i][:], mybir.AluOpType.subtract)
+            nc.vector.tensor_tensor(diff[:], table[:].indirect(entries), queries[i][:], ALU.subtract)
+            return diff
+
+        def weighted_sum(x, width):
+            dist = psum.tile([P, width], F32, name="dist")
+            nc.tensor.matmul(dist[:], weights[:], x[:], start=True, stop=True)
+            return dist
+
+        def finish(dist, start, width):
+            result = work.tile([P, width], F32, name="result")
+            nc.scalar.activation(result[:], dist[:], ACT.Exp, scale=-1.0)
+            nc.sync.dma_start(out[:, start:start + width], result[:])
+
+        dists = []
+        for i in range(last):
+            diff = difference(i)
             x = work.tile([P, PIECE], BF16, name="x")
             nc.scalar.activation(x[:], diff[:], ACT.Abs)
-            dist = psum.tile([P, PIECE], F32, name="dist")
-            nc.tensor.matmul(dist[:], weights[:], x[:], start=True, stop=True)
-            result = work.tile([P, PIECE], F32, name="result")
-            nc.scalar.activation(result[:], dist[:], ACT.Exp, scale=-1.0)
-            nc.sync.dma_start(out[:, i * PIECE:(i + 1) * PIECE], result[:])
+            dists.append(weighted_sum(x, PIECE))
+            if i > 0:
+                finish(dists[i - 1], (i - 1) * PIECE, PIECE)
+        finish(dists[last - 1], (last - 1) * PIECE, PIECE)
+
+        diff = difference(last)
+        for h in range(2):
+            part = diff[:, h * HALF:(h + 1) * HALF]
+            x = work.tile([P, HALF], BF16, name="x")
+            nc.vector.scalar_tensor_tensor(x[:], part, -1.0, part, ALU.mult, ALU.max)
+            finish(weighted_sum(x, HALF), last * PIECE + h * HALF, HALF)

@@ -17,14 +17,16 @@ def tile_lookup_manh_sub_rbf_kernel(tc, tab, qry, w, offs, out):
     last = pieces - 1
     with (
         tc.tile_pool(name="held", bufs=1) as held,
-        tc.tile_pool(name="work", bufs=pieces + 1) as work,
-        tc.psum_pool(name="psum", bufs=pieces + 1) as psum,
+        tc.tile_pool(name="work", bufs=2 * pieces) as work,
+        tc.psum_pool(name="psum", bufs=2 * pieces) as psum,
     ):
         offsets = held.tile([P, N // GROUP], U16, name="offsets")
         table = held.tile([P, tab.shape[1]], F32, name="table")
         weights = held.tile([P, P], BF16, name="weights")
         queries = [work.tile([P, PIECE], F32, name="query") for i in range(pieces)]
-        nc.sync.dma_start(table[:], tab)
+        middle = tab.shape[1] // 2
+        nc.sync.dma_start(table[:, :middle], tab[:, :middle])
+        nc.scalar.dma_start(table[:, middle:], tab[:, middle:])
         nc.sync.dma_start(offsets[:], offs)
         nc.sync.dma_start(queries[0][:], qry[:, 0:PIECE])
         nc.sync.dma_start(weights[:], w)
@@ -37,29 +39,25 @@ def tile_lookup_manh_sub_rbf_kernel(tc, tab, qry, w, offs, out):
             nc.vector.tensor_tensor(diff[:], table[:].indirect(entries), queries[i][:], ALU.subtract)
             return diff
 
-        def weighted_sum(x, width):
-            dist = psum.tile([P, width], F32, name="dist")
-            nc.tensor.matmul(dist[:], weights[:], x[:], start=True, stop=True)
-            return dist
-
-        def finish(dist, start, width):
-            result = work.tile([P, width], F32, name="result")
-            nc.scalar.activation(result[:], dist[:], ACT.Exp, scale=-1.0)
-            nc.sync.dma_start(out[:, start:start + width], result[:])
-
-        dists = []
-        for i in range(last):
-            diff = difference(i)
-            x = work.tile([P, PIECE], BF16, name="x")
-            nc.scalar.activation(x[:], diff[:], ACT.Abs)
-            dists.append(weighted_sum(x, PIECE))
-            if i > 0:
-                finish(dists[i - 1], (i - 1) * PIECE, PIECE)
-        finish(dists[last - 1], (last - 1) * PIECE, PIECE)
-
-        diff = difference(last)
-        for h in range(2):
-            part = diff[:, h * HALF:(h + 1) * HALF]
+        def absolute(part, on_vector):
             x = work.tile([P, HALF], BF16, name="x")
-            nc.vector.scalar_tensor_tensor(x[:], part, -1.0, part, ALU.mult, ALU.max)
-            finish(weighted_sum(x, HALF), last * PIECE + h * HALF, HALF)
+            if on_vector:
+                nc.vector.scalar_tensor_tensor(x[:], part, -1.0, part, ALU.mult, ALU.max)
+            else:
+                nc.scalar.activation(x[:], part, ACT.Abs)
+            return x
+
+        for i in range(pieces):
+            diff = difference(i)
+            dists = []
+            for h in range(2):
+                x = absolute(diff[:, h * HALF:(h + 1) * HALF], on_vector=(i == last))
+                dist = psum.tile([P, HALF], F32, name="dist")
+                nc.tensor.matmul(dist[:], weights[:], x[:], start=True, stop=True)
+                dists.append(dist)
+            for h in range(2):
+                result = work.tile([P, HALF], F32, name="result")
+                nc.scalar.activation(result[:], dists[h][:], ACT.Exp, scale=-1.0)
+                start = i * PIECE + h * HALF
+                queue = nc.scalar if start + HALF == N else nc.sync
+                queue.dma_start(out[:, start:start + HALF], result[:])

import concourse.mybir as mybir

P = 128
N = 2048
PIECE = 512
HALF = PIECE // 2
GROUP = 16
F32, BF16, U16 = mybir.dt.float32, mybir.dt.bfloat16, mybir.dt.uint16
ACT = mybir.ActivationFunctionType
ALU = mybir.AluOpType
FLOPS = 2 * P * P * N


def tile_lookup_manh_sub_rbf_kernel(tc, tab, qry, w, offs, out):
    nc = tc.nc
    pieces = N // PIECE
    last = pieces - 1
    with (
        tc.tile_pool(name="held", bufs=1) as held,
        tc.tile_pool(name="work", bufs=2 * pieces) as work,
        tc.psum_pool(name="psum", bufs=2 * pieces) as psum,
    ):
        offsets = held.tile([P, N // GROUP], U16, name="offsets")
        table = held.tile([P, tab.shape[1]], F32, name="table")
        weights = held.tile([P, P], BF16, name="weights")
        queries = [work.tile([P, PIECE], F32, name="query") for i in range(pieces)]
        middle = tab.shape[1] // 2
        nc.sync.dma_start(table[:, :middle], tab[:, :middle])
        nc.scalar.dma_start(table[:, middle:], tab[:, middle:])
        nc.sync.dma_start(offsets[:], offs)
        nc.sync.dma_start(queries[0][:], qry[:, 0:PIECE])
        nc.sync.dma_start(weights[:], w)
        for i in range(1, pieces):
            nc.sync.dma_start(queries[i][:], qry[:, i * PIECE:(i + 1) * PIECE])

        def difference(i):
            entries = offsets[:, i * PIECE // GROUP:(i + 1) * PIECE // GROUP]
            diff = work.tile([P, PIECE], F32, name="diff")
            nc.vector.tensor_tensor(diff[:], table[:].indirect(entries), queries[i][:], ALU.subtract)
            return diff

        def absolute(part, on_vector):
            x = work.tile([P, HALF], BF16, name="x")
            if on_vector:
                nc.vector.scalar_tensor_tensor(x[:], part, -1.0, part, ALU.mult, ALU.max)
            else:
                nc.scalar.activation(x[:], part, ACT.Abs)
            return x

        for i in range(pieces):
            diff = difference(i)
            dists = []
            for h in range(2):
                x = absolute(diff[:, h * HALF:(h + 1) * HALF], on_vector=(i == last))
                dist = psum.tile([P, HALF], F32, name="dist")
                nc.tensor.matmul(dist[:], weights[:], x[:], start=True, stop=True)
                dists.append(dist)
            for h in range(2):
                result = work.tile([P, HALF], F32, name="result")
                nc.scalar.activation(result[:], dists[h][:], ACT.Exp, scale=-1.0)
                start = i * PIECE + h * HALF
                queue = nc.scalar if start + HALF == N else nc.sync
                queue.dma_start(out[:, start:start + HALF], result[:])
